import numpy as np, ml_dtypes
CORES = [4,12,20,28,44,60,76,84,92,108,116,124]
N = 12
import mx_ref
NC, G = 256, 4
EPS = 0.001
BF = ml_dtypes.bfloat16
def cut(t, i, w=512):
    return t[:, w * i:w * i + w]
def tile(rs):
    return np.stack(rs, axis=2).reshape(128, -1).astype(BF)
def layer(w, X):
    out = []
    for i in range(G):
        for t in range(len(X)):
            p = mx_ref.matmul(mx_ref.quantize(cut(w, len(X) * i + t)), X[t])
            z = p if t == 0 else z + p
        out.append(z)
    return out
def normed(Z, s):
    return [z * f for z, f in zip(Z, s)]
def setup_inputs(rng):
    def f(*shape):
        return mx_ref.flush((rng.standard_normal(shape, dtype=np.float32) * np.exp2(rng.integers(-2, 3, shape[:-1] + (1,)))).astype(BF))
    return {"x": f(N, 128, 4 * NC), "w1": f(N, 128, G * 512), "w2": f(N, 128, 2 * 512)}
def setup_inputs_blocks(rng):
    d = setup_inputs(rng)
    for k in ("x", "w1", "w2"): d[k] = mx_ref.spread(d[k], rng, 4)
    return d
def setup_inputs_wide(rng):
    d = setup_inputs(rng)
    for k in ("x", "w1", "w2"): d[k] = mx_ref.flush((d[k].astype(np.float32) * np.exp2(rng.integers(-5, 6, (N, 1, 1))).astype(np.float32)).astype(BF))
    return d
def setup_inputs_rows(rng):
    d = setup_inputs(rng); v = d["w1"].astype(np.float32).reshape(N, 128, -1, 4)
    d["w1"] = mx_ref.flush((v * np.exp2(rng.integers(-6, 7, (N, 1, v.shape[2], 1))).astype(np.float32)).reshape(d["w1"].shape).astype(BF))
    return d
def setup_inputs_faint(rng):
    d = setup_inputs(rng); d["x"] = mx_ref.flush((d["x"].astype(np.float32) * np.float32(2.0 ** -12)).astype(BF))
    return d
def reference(x, w1, w2, own=None):
    Z = [layer(w1[r], [mx_ref.quantize(x[r])]) for r in range(N)]
    ms = [sum((Z[r][i].astype(np.float64) ** 2).sum(axis=1, keepdims=True) for r in range(N)) / (N * NC) for i in range(G)]
    s = [(1 / np.sqrt(m + EPS)).astype(np.float32) for m in ms]
    h = np.stack([tile(normed(Z[r], s)) for r in range(N)])
    use = h if own is None else own["h"]
    H = [mx_ref.quantize(use[j]) for j in range(N)]
    y = np.zeros((N, 128, NC), np.float32)
    for r in range(N):
        y[r] = mx_ref.matmul(mx_ref.quantize(cut(w2[r], 0)), H[r]) + mx_ref.matmul(mx_ref.quantize(cut(w2[r], 1)), H[(r + 1) % N])
    return {"h": h, "y": y}

@@ -1,0 +1,235 @@
+from concourse.bass import DstId, RemoteDMATransfer
+from concourse.mybir import dt, AluOpType, AxisListType, ActivationFunctionType
+
+NC, G = 256, 4
+EPS = 0.001
+SIM_CORES = 128
+HALF = NC // 2
+
+SCRATCH = {
+    "xb": ("sbuf", [128, 4 * NC], "bfloat16"),
+    "w1b": ("sbuf", [128, G * 512], "bfloat16"),
+    "w2b": ("sbuf", [128, 2 * 512], "bfloat16"),
+    "xq": ("sbuf", [128, NC], "float8_e4m3fn_x4"), "xsc": ("sbuf", [128, NC], "uint8"),
+    "w1q": ("sbuf", [128, G * 128], "float8_e4m3fn_x4"), "w1sc": ("sbuf", [128, G * 128], "uint8"),
+    "w2q": ("sbuf", [128, 2 * 128], "float8_e4m3fn_x4"), "w2sc": ("sbuf", [128, 2 * 128], "uint8"),
+    "zp": ("psum", [128, G * 512], "float32"),
+    "yp": ("psum", [128, 2 * 512], "float32"),
+    "sqj": ("sbuf", [128, G * NC], "float32"),
+    "land": ("sbuf", [128, 4 * 12], "float32"),
+    "rj": ("sbuf", [128, 2 * 12], "float32"),
+    "tot": ("sbuf", [128, G], "float32"),
+    "rt": ("sbuf", [128, G], "float32"),
+    "av": ("sbuf", [128, G], "float32"),
+    "q0": ("sbuf", [128, G], "float32"),
+    "t1": ("sbuf", [128, G], "float32"),
+    "t2": ("sbuf", [128, G], "float32"),
+    "t3": ("sbuf", [128, G], "float32"),
+    "sv": ("sbuf", [128, G], "float32"),
+    "hb": ("sbuf", [128, 4 * NC], "bfloat16"),
+    "hq": ("sbuf", [128, NC], "float8_e4m3fn_x4"), "hsc": ("sbuf", [128, NC], "uint8"),
+    "nq": ("sbuf", [128, NC], "float8_e4m3fn_x4"), "nsc": ("sbuf", [128, NC], "uint8"),
+    "ysb": ("sbuf", [128, NC], "float32"),
+}
+SEMAPHORES = (["ld_x", "ld_w2", "q_x", "q_w2", "sq", "ssin", "snt", "arr", "redv", "reds", "rts", "avs",
+               "n1", "n2", "n3", "sready", "hsn", "c0", "c1", "sc", "y0", "y1", "yc", "st_h", "st_y"]
+              + ["ld_w1_%d" % i for i in range(G)] + ["q_w1_%d" % i for i in range(G)] + ["mm_%d" % i for i in range(G)]
+              + ["hv_%d" % k for k in range(2)] + ["ha_%d" % k for k in range(2)] + ["q_h_%d" % k for k in range(2)])
+
+
+def _bits(m):
+    return bin(m).count("1")
+
+
+def _plan(T, topo):
+    cores = list(T.cores)
+    n = len(cores)
+    plan = []
+    for r, c in enumerate(cores):
+        others = [d for d in cores if d != c]
+        ports = [k for k in range(SIM_CORES)
+                 if topo.chip(k) == topo.chip(c) and k not in cores and all(topo.may_write(k, d) for d in others)]
+        near = [k for k in ports if topo.die(k) == topo.die(c)]
+        far = [k for k in ports if topo.die(k) != topo.die(c)]
+        helpers = near + far
+        direct = [d for d in others if topo.may_write(c, d)][:3]
+        rest = [d for d in others if d not in direct]
+        share = {h: rest[i::len(helpers)] for i, h in enumerate(helpers)}
+        to = cores[(r - 1) % n]
+        if topo.may_write(c, to):
+            via = {"c0": None, "c1": None, "sc": None}
+        else:
+            via = {"c0": far[0], "c1": near[0], "sc": far[1]}
+        plan.append({"core": c, "helpers": helpers, "direct": direct, "share": share, "to": to, "via": via})
+    return plan
+
+
+def _fan(g, topo, src_core, dsts, ap, remote_sem, local_sem):
+    m = topo.mask(src_core, dsts[0])
+    for d in dsts:
+        m &= topo.mask(src_core, d)
+    ids = [DstId(rid=topo.addr(d)[0], pnc=topo.addr(d)[1]) for d in dsts]
+    g.remote_dma_fused([RemoteDMATransfer(dst_ids=ids, dma_engine_mask=m, remote_sem=remote_sem,
+                                          srcs=[ap], dsts=[ap for _ in dsts])], local_sem=local_sem)
+    return _bits(m)
+
+
+def _send(g, topo, src_core, dst_core, out_ap, in_ap, remote_sem, local_sem):
+    rid, pid = topo.addr(dst_core)[:2]
+    m = topo.mask(src_core, dst_core)
+    g.remote_dma(out_ap, in_ap, remote_sem, local_sem, pid, rid, m)
+    return _bits(m)
+
+
+def _piece(T, buf_q, buf_s, name):
+    if name == "c0":
+        return T[buf_q][:, 0:HALF].bitcast(dt.uint8)
+    if name == "c1":
+        return T[buf_q][:, HALF:NC].bitcast(dt.uint8)
+    return T[buf_s][:]
+
+
+def _helper(g, core, T, topo, plan):
+    S = T.sem
+    for r, p in enumerate(plan):
+        if core not in p["helpers"]:
+            continue
+        left = 0
+        g.wait_ge(S.ssin, _bits(topo.mask(p["core"], core)))
+        left += _fan(g, topo, core, p["share"][core], T.land[:, 4 * r:4 * r + 4], S.arr, S.snt)
+        for name in ("c0", "c1", "sc"):
+            if p["via"][name] == core:
+                g.wait_ge(S[name], _bits(topo.mask(p["core"], core)))
+                ap = _piece(T, "nq", "nsc", name)
+                left += _send(g, topo, core, p["to"], ap, ap, S[name], S.snt)
+        g.wait_ge(S.snt, left)
+
+
+def rank_program(g, core, T, topo):
+    plan = _plan(T, topo)
+    rank = T.rank_of(core)
+    if rank is None:
+        _helper(g, core, T, topo, plan)
+        return
+    S = T.sem
+    p = plan[rank]
+    n = len(plan)
+    v, s, t, y = g.vector, g.scalar, g.tensor, g.sync
+    mult, add = AluOpType.mult, AluOpType.add
+    Act = ActivationFunctionType
+
+    arr = 0
+    for q in plan:
+        if core in q["direct"]:
+            arr += _bits(topo.mask(q["core"], core))
+        for h in q["helpers"]:
+            if core in q["share"][h]:
+                arr += _bits(topo.mask(h, core))
+    src = plan[(rank + 1) % n]
+    got = {k: _bits(topo.mask(src["via"][k] if src["via"][k] is not None else src["core"], core)) for k in ("c0", "c1", "sc")}
+
+    def w1_load(q, i):
+        q.dma_start(T.w1b[:, 512 * i:512 * i + 512], T.w1[:, 512 * i:512 * i + 512]).then_inc(S["ld_w1_%d" % i], 16)
+    y.dma_start(T.xb[:], T.x[:]).then_inc(S.ld_x, 16)
+    w1_load(s, 0)
+    w1_load(y, 1)
+    w1_load(s, 2)
+    w1_load(y, 3)
+
+    v.wait_ge(S.ld_x, 16)
+    v.quantize_mx(T.xq[:], T.xsc[:], T.xb[:]).then_inc(S.q_x, 1)
+    t.wait_ge(S.q_x, 1)
+    own = 4 * rank
+    for i in range(G):
+        v.wait_ge(S["ld_w1_%d" % i], 16)
+        v.quantize_mx(T.w1q[:, 128 * i:128 * i + 128], T.w1sc[:, 128 * i:128 * i + 128],
+                      T.w1b[:, 512 * i:512 * i + 512]).then_inc(S["q_w1_%d" % i], 1)
+        t.wait_ge(S["q_w1_%d" % i], 1)
+        t.matmul_mx(T.zp[:, 512 * i:512 * i + NC], T.w1q[:, 128 * i:128 * i + 128], T.w1sc[:, 128 * i:128 * i + 128],
+                    T.xq[:], T.xsc[:], True, True).then_inc(S["mm_%d" % i], 1)
+        s.wait_ge(S["mm_%d" % i], 1)
+        s.activation(T.sqj[:, NC * i:NC * i + NC], T.zp[:, 512 * i:512 * i + NC], Act.Square,
+                     accum_out=T.land[:, own + i:own + i + 1]).then_inc(S.sq, 1)
+
+    g.wait_ge(S.sq, G)
+    slot = T.land[:, own:own + 4]
+    left = _fan(g, topo, core, p["helpers"], slot, S.ssin, S.snt)
+    left += _fan(g, topo, core, p["direct"], slot, S.arr, S.snt)
+    y.wait_ge(S.snt, left)
+    y.dma_start(T.w2b[:], T.w2[:]).then_inc(S.ld_w2, 16)
+
+    inv = 1.0 / float(n * NC)
+    v.wait_ge(S.sq, G)
+    v.wait_ge(S.arr, arr)
+    s.wait_ge(S.sq, G)
+    s.wait_ge(S.arr, arr)
+    for i in (0, 1):
+        v.tensor_reduce(T.tot[:, i:i + 1], T.land[:, i:4 * n:4], AxisListType.X, add).then_inc(S.redv, 1)
+    for i in (2, 3):
+        s.activation(T.rj[:, n * (i - 2):n * (i - 1)], T.land[:, i:4 * n:4], Act.Copy,
+                     accum_out=T.tot[:, i:i + 1]).then_inc(S.reds, 1)
+    for q in (v, s):
+        q.wait_ge(S.redv, 2)
+        q.wait_ge(S.reds, 2)
+    s.activation(T.rt[:], T.tot[:], Act.Sqrt, bias=EPS, scale=inv).then_inc(S.rts, 1)
+    v.tensor_scalar(T.av[:], T.tot[:], inv, EPS, mult, add).then_inc(S.avs, 1)
+    v.wait_ge(S.rts, 1)
+    v.reciprocal(T.q0[:], T.rt[:]).then_inc(S.n1, 1)
+    v.wait_ge(S.n1, 1)
+    v.wait_ge(S.avs, 1)
+    v.tensor_tensor(T.t1[:], T.av[:], T.q0[:], mult).then_inc(S.n2, 1)
+    v.wait_ge(S.n2, 1)
+    v.tensor_tensor(T.t2[:], T.t1[:], T.q0[:], mult).then_inc(S.n3, 1)
+    v.wait_ge(S.n3, 1)
+    v.tensor_scalar(T.t3[:], T.t2[:], -0.5, 1.5, mult, add).then_inc(S.n3, 1)
+    v.wait_ge(S.n3, 2)
+    v.tensor_tensor(T.sv[:], T.q0[:], T.t3[:], mult).then_inc(S.sready, 1)
+    v.wait_ge(S.sready, 1)
+    s.wait_ge(S.sready, 1)
+
+    sent = 0
+    for k in range(2):
+        for b in range(G):
+            out = T.hb[:, 512 * k + b:512 * k + 512:4]
+            z = T.zp[:, 512 * b + HALF * k:512 * b + HALF * k + HALF]
+            if b < 2:
+                v.tensor_scalar(out, z, T.sv[:, b:b + 1], None, mult).then_inc(S["hv_%d" % k], 1)
+            else:
+                s.activation(out, z, Act.Copy, scale=T.sv[:, b:b + 1]).then_inc(S["ha_%d" % k], 1)
+        v.wait_ge(S["hv_%d" % k], 2)
+        v.wait_ge(S["ha_%d" % k], 2)
+        v.quantize_mx(T.hq[:, HALF * k:HALF * k + HALF], T.hsc[:, HALF * k:HALF * k + HALF],
+                      T.hb[:, 512 * k:512 * k + 512]).then_inc(S["q_h_%d" % k], 1)
+        g.wait_ge(S["q_h_%d" % k], 1)
+        for name in (("c0",), ("c1", "sc"))[k]:
+            dst = p["via"][name] if p["via"][name] is not None else p["to"]
+            sent += _send(g, topo, core, dst, _piece(T, "nq", "nsc", name), _piece(T, "hq", "hsc", name), S[name], S.hsn)
+
+    for k in range(2):
+        y.wait_ge(S["hv_%d" % k], 2)
+        y.wait_ge(S["ha_%d" % k], 2)
+    y.wait_ge(S.hsn, sent)
+    y.dma_start(T.h[:], T.hb[:]).then_inc(S.st_h, 16)
+
+    v.wait_ge(S.ld_w2, 16)
+    for i in range(2):
+        v.quantize_mx(T.w2q[:, 128 * i:128 * i + 128], T.w2sc[:, 128 * i:128 * i + 128],
+                      T.w2b[:, 512 * i:512 * i + 512]).then_inc(S.q_w2, 1)
+    t.wait_ge(S.q_w2, 2)
+    for k in range(2):
+        t.wait_ge(S["q_h_%d" % k], 1)
+        t.matmul_mx(T.yp[:, 512 * k:512 * k + HALF], T.w2q[:, 0:128], T.w2sc[:, 0:128],
+                    T.hq[:, HALF * k:HALF * k + HALF], T.hsc[:, HALF * k:HALF * k + HALF], True, False)
+    t.wait_ge(S.sc, got["sc"])
+    for k in range(2):
+        t.wait_ge(S["c%d" % k], got["c%d" % k])
+        t.matmul_mx(T.yp[:, 512 * k:512 * k + HALF], T.w2q[:, 128:256], T.w2sc[:, 128:256],
+                    T.nq[:, HALF * k:HALF * k + HALF], T.nsc[:, HALF * k:HALF * k + HALF], False, True).then_inc(S["y%d" % k], 1)
+    v.wait_ge(S.y0, 1)
+    v.tensor_copy(T.ysb[:, 0:HALF], T.yp[:, 0:HALF]).then_inc(S.yc, 1)
+    s.wait_ge(S.y1, 1)
+    s.activation(T.ysb[:, HALF:NC], T.yp[:, 512:512 + HALF], Act.Copy).then_inc(S.yc, 1)
+    y.wait_ge(S.yc, 2)
+    y.dma_start(T.y[:], T.ysb[:]).then_inc(S.st_y, 16)
+    y.wait_ge(S.st_h, 16)
+    y.wait_ge(S.st_y, 16)

@@ -17,7 +17,7 @@ SCRATCH = {
     "yp": ("psum", [128, 2 * 512], "float32"),
     "sqj": ("sbuf", [128, G * NC], "float32"),
     "land": ("sbuf", [128, 4 * 12], "float32"),
-    "rj": ("sbuf", [128, 2 * 12], "float32"),
+    "rj": ("sbuf", [128, 12], "float32"),
     "tot": ("sbuf", [128, G], "float32"),
     "rt": ("sbuf", [128, G], "float32"),
     "av": ("sbuf", [128, G], "float32"),
@@ -31,8 +31,8 @@ SCRATCH = {
     "nq": ("sbuf", [128, NC], "float8_e4m3fn_x4"), "nsc": ("sbuf", [128, NC], "uint8"),
     "ysb": ("sbuf", [128, NC], "float32"),
 }
-SEMAPHORES = (["ld_x", "ld_w2", "q_x", "q_w2", "sq", "ssin", "snt", "arr", "redv", "reds", "rts", "avs",
-               "n1", "n2", "n3", "sready", "hsn", "c0", "c1", "sc", "y0", "y1", "yc", "st_h", "st_y"]
+SEMAPHORES = (["ld_x", "ld_w2", "q_x", "q_w2", "sqa", "sq", "ssin0", "ssin1", "snt", "arr0", "arr1", "red0", "redv", "rts",
+               "avs", "n1", "n2", "n3", "sready", "hsn", "c0", "c1", "sc", "y0", "y1", "yc", "st_h", "st_y"]
               + ["ld_w1_%d" % i for i in range(G)] + ["q_w1_%d" % i for i in range(G)] + ["mm_%d" % i for i in range(G)]
               + ["hv_%d" % k for k in range(2)] + ["ha_%d" % k for k in range(2)] + ["q_h_%d" % k for k in range(2)])
 
@@ -95,8 +95,10 @@ def _helper(g, core, T, topo, plan):
         if core not in p["helpers"]:
             continue
         left = 0
-        g.wait_ge(S.ssin, _bits(topo.mask(p["core"], core)))
-        left += _fan(g, topo, core, p["share"][core], T.land[:, 4 * r:4 * r + 4], S.arr, S.snt)
+        g.wait_ge(S.ssin0, _bits(topo.mask(p["core"], core)))
+        left += _fan(g, topo, core, p["share"][core], T.land[:, 4 * r:4 * r + 1], S.arr0, S.snt)
+        g.wait_ge(S.ssin1, _bits(topo.mask(p["core"], core)))
+        left += _fan(g, topo, core, p["share"][core], T.land[:, 4 * r + 1:4 * r + 4], S.arr1, S.snt)
         for name in ("c0", "c1", "sc"):
             if p["via"][name] == core:
                 g.wait_ge(S[name], _bits(topo.mask(p["core"], core)))
@@ -149,31 +151,33 @@ def rank_program(g, core, T, topo):
                     T.xq[:], T.xsc[:], True, True).then_inc(S["mm_%d" % i], 1)
         s.wait_ge(S["mm_%d" % i], 1)
         s.activation(T.sqj[:, NC * i:NC * i + NC], T.zp[:, 512 * i:512 * i + NC], Act.Square,
-                     accum_out=T.land[:, own + i:own + i + 1]).then_inc(S.sq, 1)
+                     accum_out=T.land[:, own + i:own + i + 1]).then_inc(S.sqa if i == 0 else S.sq, 1)
 
-    g.wait_ge(S.sq, G)
-    slot = T.land[:, own:own + 4]
-    left = _fan(g, topo, core, p["helpers"], slot, S.ssin, S.snt)
-    left += _fan(g, topo, core, p["direct"], slot, S.arr, S.snt)
+    g.wait_ge(S.sqa, 1)
+    left = _fan(g, topo, core, p["helpers"], T.land[:, own:own + 1], S.ssin0, S.snt)
+    left += _fan(g, topo, core, p["direct"], T.land[:, own:own + 1], S.arr0, S.snt)
+    g.wait_ge(S.sq, G - 1)
+    left += _fan(g, topo, core, p["helpers"], T.land[:, own + 1:own + 4], S.ssin1, S.snt)
+    left += _fan(g, topo, core, p["direct"], T.land[:, own + 1:own + 4], S.arr1, S.snt)
     y.wait_ge(S.snt, left)
     y.dma_start(T.w2b[:], T.w2[:]).then_inc(S.ld_w2, 16)
 
     inv = 1.0 / float(n * NC)
-    v.wait_ge(S.sq, G)
-    v.wait_ge(S.arr, arr)
-    s.wait_ge(S.sq, G)
-    s.wait_ge(S.arr, arr)
-    for i in (0, 1):
+    s.wait_ge(S.sqa, 1)
+    s.wait_ge(S.arr0, arr)
+    s.activation(T.rj[:], T.land[:, 0:4 * n:4], Act.Copy, accum_out=T.tot[:, 0:1]).then_inc(S.red0, 1)
+    s.wait_ge(S.red0, 1)
+    s.activation(T.rt[:, 0:1], T.tot[:, 0:1], Act.Sqrt, bias=EPS, scale=inv).then_inc(S.rts, 1)
+    v.wait_ge(S.sq, G - 1)
+    v.wait_ge(S.arr1, arr)
+    for i in range(1, G):
         v.tensor_reduce(T.tot[:, i:i + 1], T.land[:, i:4 * n:4], AxisListType.X, add).then_inc(S.redv, 1)
-    for i in (2, 3):
-        s.activation(T.rj[:, n * (i - 2):n * (i - 1)], T.land[:, i:4 * n:4], Act.Copy,
-                     accum_out=T.tot[:, i:i + 1]).then_inc(S.reds, 1)
-    for q in (v, s):
-        q.wait_ge(S.redv, 2)
-        q.wait_ge(S.reds, 2)
-    s.activation(T.rt[:], T.tot[:], Act.Sqrt, bias=EPS, scale=inv).then_inc(S.rts, 1)
+    s.wait_ge(S.redv, G - 1)
+    s.activation(T.rt[:, 1:G], T.tot[:, 1:G], Act.Sqrt, bias=EPS, scale=inv).then_inc(S.rts, 1)
+    v.wait_ge(S.redv, G - 1)
+    v.wait_ge(S.red0, 1)
     v.tensor_scalar(T.av[:], T.tot[:], inv, EPS, mult, add).then_inc(S.avs, 1)
-    v.wait_ge(S.rts, 1)
+    v.wait_ge(S.rts, 2)
     v.reciprocal(T.q0[:], T.rt[:]).then_inc(S.n1, 1)
     v.wait_ge(S.n1, 1)
     v.wait_ge(S.avs, 1)

@@ -5,6 +5,8 @@ NC, G = 256, 4
 EPS = 0.001
 SIM_CORES = 128
 HALF = NC // 2
+NR = 12
+PIECES = ("c0", "s0", "c1", "s1")
 
 SCRATCH = {
     "xb": ("sbuf", [128, 4 * NC], "bfloat16"),
@@ -16,23 +18,24 @@ SCRATCH = {
     "zp": ("psum", [128, G * 512], "float32"),
     "yp": ("psum", [128, 2 * 512], "float32"),
     "sqj": ("sbuf", [128, G * NC], "float32"),
-    "land": ("sbuf", [128, 4 * 12], "float32"),
-    "rj": ("sbuf", [128, 12], "float32"),
+    "land": ("sbuf", [128, 4 * (NR + 1)], "float32"),
+    "rj": ("sbuf", [128, NR + 1], "float32"),
     "tot": ("sbuf", [128, G], "float32"),
     "rt": ("sbuf", [128, G], "float32"),
-    "av": ("sbuf", [128, G], "float32"),
-    "q0": ("sbuf", [128, G], "float32"),
-    "t1": ("sbuf", [128, G], "float32"),
-    "t2": ("sbuf", [128, G], "float32"),
-    "t3": ("sbuf", [128, G], "float32"),
+    "ra": ("sbuf", [128, G], "float32"),
+    "uu": ("sbuf", [128, G], "float32"),
+    "ww": ("sbuf", [128, G], "float32"),
+    "tt": ("sbuf", [128, G], "float32"),
     "sv": ("sbuf", [128, G], "float32"),
     "hb": ("sbuf", [128, 4 * NC], "bfloat16"),
     "hq": ("sbuf", [128, NC], "float8_e4m3fn_x4"), "hsc": ("sbuf", [128, NC], "uint8"),
     "nq": ("sbuf", [128, NC], "float8_e4m3fn_x4"), "nsc": ("sbuf", [128, NC], "uint8"),
     "ysb": ("sbuf", [128, NC], "float32"),
 }
-SEMAPHORES = (["ld_x", "ld_w2", "q_x", "q_w2", "sqa", "sq", "ssin0", "ssin1", "snt", "arr0", "arr1", "red0", "redv", "rts",
-               "avs", "n1", "n2", "n3", "sready", "hsn", "c0", "c1", "sc", "y0", "y1", "yc", "st_h", "st_y"]
+SEMAPHORES = (["ld_x", "ld_w2", "q_x", "q_w2", "sqa", "sq", "ssin0", "ssin1", "snt", "arr0", "arr1", "cst", "red0", "redv",
+               "rts", "n1", "n2", "n3", "n4", "sready", "hsn", "in0", "in1", "y0", "y1", "yc0", "yc1",
+               "st_h", "st_y0", "st_y1"]
+              + ["p_" + k for k in PIECES]
               + ["ld_w1_%d" % i for i in range(G)] + ["q_w1_%d" % i for i in range(G)] + ["mm_%d" % i for i in range(G)]
               + ["hv_%d" % k for k in range(2)] + ["ha_%d" % k for k in range(2)] + ["q_h_%d" % k for k in range(2)])
 
@@ -57,9 +60,9 @@ def _plan(T, topo):
         share = {h: rest[i::len(helpers)] for i, h in enumerate(helpers)}
         to = cores[(r - 1) % n]
         if topo.may_write(c, to):
-            via = {"c0": None, "c1": None, "sc": None}
+            via = {"c0": far[0], "s0": far[1], "c1": None, "s1": None}
         else:
-            via = {"c0": far[0], "c1": near[0], "sc": far[1]}
+            via = {"c0": far[0], "s0": far[1], "c1": near[0], "s1": near[1]}
         plan.append({"core": c, "helpers": helpers, "direct": direct, "share": share, "to": to, "via": via})
     return plan
 
@@ -82,11 +85,10 @@ def _send(g, topo, src_core, dst_core, out_ap, in_ap, remote_sem, local_sem):
 
 
 def _piece(T, buf_q, buf_s, name):
-    if name == "c0":
-        return T[buf_q][:, 0:HALF].bitcast(dt.uint8)
-    if name == "c1":
-        return T[buf_q][:, HALF:NC].bitcast(dt.uint8)
-    return T[buf_s][:]
+    k = int(name[1])
+    if name[0] == "c":
+        return T[buf_q][:, HALF * k:HALF * k + HALF].bitcast(dt.uint8)
+    return T[buf_s][:, HALF * k:HALF * k + HALF]
 
 
 def _helper(g, core, T, topo, plan):
@@ -99,11 +101,11 @@ def _helper(g, core, T, topo, plan):
         left += _fan(g, topo, core, p["share"][core], T.land[:, 4 * r:4 * r + 1], S.arr0, S.snt)
         g.wait_ge(S.ssin1, _bits(topo.mask(p["core"], core)))
         left += _fan(g, topo, core, p["share"][core], T.land[:, 4 * r + 1:4 * r + 4], S.arr1, S.snt)
-        for name in ("c0", "c1", "sc"):
+        for name in PIECES:
             if p["via"][name] == core:
-                g.wait_ge(S[name], _bits(topo.mask(p["core"], core)))
+                g.wait_ge(S["p_" + name], _bits(topo.mask(p["core"], core)))
                 ap = _piece(T, "nq", "nsc", name)
-                left += _send(g, topo, core, p["to"], ap, ap, S[name], S.snt)
+                left += _send(g, topo, core, p["to"], ap, ap, S["in" + name[1]], S.snt)
         g.wait_ge(S.snt, left)
 
 
@@ -119,6 +121,7 @@ def rank_program(g, core, T, topo):
     v, s, t, y = g.vector, g.scalar, g.tensor, g.sync
     mult, add = AluOpType.mult, AluOpType.add
     Act = ActivationFunctionType
+    W = 4 * (n + 1)
 
     arr = 0
     for q in plan:
@@ -128,7 +131,9 @@ def rank_program(g, core, T, topo):
             if core in q["share"][h]:
                 arr += _bits(topo.mask(h, core))
     src = plan[(rank + 1) % n]
-    got = {k: _bits(topo.mask(src["via"][k] if src["via"][k] is not None else src["core"], core)) for k in ("c0", "c1", "sc")}
+    got = [0, 0]
+    for name in PIECES:
+        got[int(name[1])] += _bits(topo.mask(src["via"][name] if src["via"][name] is not None else src["core"], core))
 
     def w1_load(q, i):
         q.dma_start(T.w1b[:, 512 * i:512 * i + 512], T.w1[:, 512 * i:512 * i + 512]).then_inc(S["ld_w1_%d" % i], 16)
@@ -138,6 +143,8 @@ def rank_program(g, core, T, topo):
     w1_load(s, 2)
     w1_load(y, 3)
 
+    cnt = float(n * NC)
+    v.memset(T.land[:, 4 * n:W], EPS * cnt).then_inc(S.cst, 1)
     v.wait_ge(S.ld_x, 16)
     v.quantize_mx(T.xq[:], T.xsc[:], T.xb[:]).then_inc(S.q_x, 1)
     t.wait_ge(S.q_x, 1)
@@ -162,32 +169,32 @@ def rank_program(g, core, T, topo):
     y.wait_ge(S.snt, left)
     y.dma_start(T.w2b[:], T.w2[:]).then_inc(S.ld_w2, 16)
 
-    inv = 1.0 / float(n * NC)
+    inv = 1.0 / cnt
     s.wait_ge(S.sqa, 1)
+    s.wait_ge(S.cst, 1)
     s.wait_ge(S.arr0, arr)
-    s.activation(T.rj[:], T.land[:, 0:4 * n:4], Act.Copy, accum_out=T.tot[:, 0:1]).then_inc(S.red0, 1)
+    s.activation(T.rj[:], T.land[:, 0:W:4], Act.Copy, accum_out=T.tot[:, 0:1]).then_inc(S.red0, 1)
     s.wait_ge(S.red0, 1)
-    s.activation(T.rt[:, 0:1], T.tot[:, 0:1], Act.Sqrt, bias=EPS, scale=inv).then_inc(S.rts, 1)
+    s.activation(T.rt[:, 0:1], T.tot[:, 0:1], Act.Sqrt, scale=inv).then_inc(S.rts, 1)
+    v.wait_ge(S.cst, 1)
     v.wait_ge(S.sq, G - 1)
     v.wait_ge(S.arr1, arr)
     for i in range(1, G):
-        v.tensor_reduce(T.tot[:, i:i + 1], T.land[:, i:4 * n:4], AxisListType.X, add).then_inc(S.redv, 1)
+        v.tensor_reduce(T.tot[:, i:i + 1], T.land[:, i:W:4], AxisListType.X, add).then_inc(S.redv, 1)
     s.wait_ge(S.redv, G - 1)
-    s.activation(T.rt[:, 1:G], T.tot[:, 1:G], Act.Sqrt, bias=EPS, scale=inv).then_inc(S.rts, 1)
+    s.activation(T.rt[:, 1:G], T.tot[:, 1:G], Act.Sqrt, scale=inv).then_inc(S.rts, 1)
     v.wait_ge(S.redv, G - 1)
     v.wait_ge(S.red0, 1)
-    v.tensor_scalar(T.av[:], T.tot[:], inv, EPS, mult, add).then_inc(S.avs, 1)
-    v.wait_ge(S.rts, 2)
-    v.reciprocal(T.q0[:], T.rt[:]).then_inc(S.n1, 1)
+    v.reciprocal(T.ra[:], T.tot[:]).then_inc(S.n1, 1)
     v.wait_ge(S.n1, 1)
-    v.wait_ge(S.avs, 1)
-    v.tensor_tensor(T.t1[:], T.av[:], T.q0[:], mult).then_inc(S.n2, 1)
+    v.wait_ge(S.rts, 2)
+    v.tensor_tensor(T.uu[:], T.rt[:], T.ra[:], mult).then_inc(S.n2, 1)
     v.wait_ge(S.n2, 1)
-    v.tensor_tensor(T.t2[:], T.t1[:], T.q0[:], mult).then_inc(S.n3, 1)
+    v.tensor_tensor(T.ww[:], T.rt[:], T.uu[:], mult).then_inc(S.n3, 1)
     v.wait_ge(S.n3, 1)
-    v.tensor_scalar(T.t3[:], T.t2[:], -0.5, 1.5, mult, add).then_inc(S.n3, 1)
-    v.wait_ge(S.n3, 2)
-    v.tensor_tensor(T.sv[:], T.q0[:], T.t3[:], mult).then_inc(S.sready, 1)
+    v.tensor_scalar(T.tt[:], T.ww[:], -0.5 * cnt * cnt, 1.5 * cnt, mult, add).then_inc(S.n4, 1)
+    v.wait_ge(S.n4, 1)
+    v.tensor_tensor(T.sv[:], T.uu[:], T.tt[:], mult).then_inc(S.sready, 1)
     v.wait_ge(S.sready, 1)
     s.wait_ge(S.sready, 1)
 
@@ -205,9 +212,12 @@ def rank_program(g, core, T, topo):
         v.quantize_mx(T.hq[:, HALF * k:HALF * k + HALF], T.hsc[:, HALF * k:HALF * k + HALF],
                       T.hb[:, 512 * k:512 * k + 512]).then_inc(S["q_h_%d" % k], 1)
         g.wait_ge(S["q_h_%d" % k], 1)
-        for name in (("c0",), ("c1", "sc"))[k]:
-            dst = p["via"][name] if p["via"][name] is not None else p["to"]
-            sent += _send(g, topo, core, dst, _piece(T, "nq", "nsc", name), _piece(T, "hq", "hsc", name), S[name], S.hsn)
+        for name in ("c%d" % k, "s%d" % k):
+            if p["via"][name] is not None:
+                dst, sem = p["via"][name], S["p_" + name]
+            else:
+                dst, sem = p["to"], S["in%d" % k]
+            sent += _send(g, topo, core, dst, _piece(T, "nq", "nsc", name), _piece(T, "hq", "hsc", name), sem, S.hsn)
 
     for k in range(2):
         y.wait_ge(S["hv_%d" % k], 2)
@@ -224,16 +234,18 @@ def rank_program(g, core, T, topo):
         t.wait_ge(S["q_h_%d" % k], 1)
         t.matmul_mx(T.yp[:, 512 * k:512 * k + HALF], T.w2q[:, 0:128], T.w2sc[:, 0:128],
                     T.hq[:, HALF * k:HALF * k + HALF], T.hsc[:, HALF * k:HALF * k + HALF], True, False)
-    t.wait_ge(S.sc, got["sc"])
     for k in range(2):
-        t.wait_ge(S["c%d" % k], got["c%d" % k])
+        t.wait_ge(S["in%d" % k], got[k])
         t.matmul_mx(T.yp[:, 512 * k:512 * k + HALF], T.w2q[:, 128:256], T.w2sc[:, 128:256],
                     T.nq[:, HALF * k:HALF * k + HALF], T.nsc[:, HALF * k:HALF * k + HALF], False, True).then_inc(S["y%d" % k], 1)
     v.wait_ge(S.y0, 1)
-    v.tensor_copy(T.ysb[:, 0:HALF], T.yp[:, 0:HALF]).then_inc(S.yc, 1)
+    v.tensor_copy(T.ysb[:, 0:HALF], T.yp[:, 0:HALF]).then_inc(S.yc0, 1)
+    y.wait_ge(S.yc0, 1)
+    y.dma_start(T.y[:, 0:HALF], T.ysb[:, 0:HALF]).then_inc(S.st_y0, 16)
     s.wait_ge(S.y1, 1)
-    s.activation(T.ysb[:, HALF:NC], T.yp[:, 512:512 + HALF], Act.Copy).then_inc(S.yc, 1)
-    y.wait_ge(S.yc, 2)
-    y.dma_start(T.y[:], T.ysb[:]).then_inc(S.st_y, 16)
+    s.activation(T.ysb[:, HALF:NC], T.yp[:, 512:512 + HALF], Act.Copy).then_inc(S.yc1, 1)
+    s.wait_ge(S.yc1, 1)
+    s.dma_start(T.y[:, HALF:NC], T.ysb[:, HALF:NC]).then_inc(S.st_y1, 16)
     y.wait_ge(S.st_h, 16)
-    y.wait_ge(S.st_y, 16)
+    y.wait_ge(S.st_y0, 16)
+    s.wait_ge(S.st_y1, 16)

@@ -6,6 +6,7 @@ EPS = 0.001
 SIM_CORES = 128
 HALF = NC // 2
 NR = 12
+SH = 2.0 ** -16
 PIECES = ("c0", "s0", "c1", "s1")
 
 SCRATCH = {
@@ -23,9 +24,6 @@ SCRATCH = {
     "tot": ("sbuf", [128, G], "float32"),
     "rt": ("sbuf", [128, G], "float32"),
     "ra": ("sbuf", [128, G], "float32"),
-    "uu": ("sbuf", [128, G], "float32"),
-    "ww": ("sbuf", [128, G], "float32"),
-    "tt": ("sbuf", [128, G], "float32"),
     "sv": ("sbuf", [128, G], "float32"),
     "hb": ("sbuf", [128, 4 * NC], "bfloat16"),
     "hq": ("sbuf", [128, NC], "float8_e4m3fn_x4"), "hsc": ("sbuf", [128, NC], "uint8"),
@@ -33,7 +31,7 @@ SCRATCH = {
     "ysb": ("sbuf", [128, NC], "float32"),
 }
 SEMAPHORES = (["ld_x", "ld_w2", "q_x", "q_w2", "sqa", "sq", "ssin0", "ssin1", "snt", "arr0", "arr1", "cst", "red0", "redv",
-               "rts", "n1", "n2", "n3", "n4", "sready", "hsn", "in0", "in1", "y0", "y1", "yc0", "yc1",
+               "rts0", "rts1", "n0", "n1", "s0r", "h0", "sready", "hsn", "in0", "in1", "y0", "y1", "yc0", "yc1",
                "st_h", "st_y0", "st_y1"]
               + ["p_" + k for k in PIECES]
               + ["ld_w1_%d" % i for i in range(G)] + ["q_w1_%d" % i for i in range(G)] + ["mm_%d" % i for i in range(G)]
@@ -44,9 +42,14 @@ def _bits(m):
     return bin(m).count("1")
 
 
+def _rows(topo, a, b):
+    return 128 // _bits(topo.mask(a, b))
+
+
 def _plan(T, topo):
     cores = list(T.cores)
     n = len(cores)
+    relayed = {c: not topo.may_write(c, cores[(r - 1) % n]) for r, c in enumerate(cores)}
     plan = []
     for r, c in enumerate(cores):
         others = [d for d in cores if d != c]
@@ -55,12 +58,19 @@ def _plan(T, topo):
         near = [k for k in ports if topo.die(k) == topo.die(c)]
         far = [k for k in ports if topo.die(k) != topo.die(c)]
         helpers = near + far
-        direct = [d for d in others if topo.may_write(c, d)][:3]
-        rest = [d for d in others if d not in direct]
-        share = {h: rest[i::len(helpers)] for i, h in enumerate(helpers)}
+        urgent = [d for d in others if relayed[d]]
+        easy = [d for d in others if not relayed[d]]
+        direct = [d for d in urgent if topo.may_write(c, d)][:3]
+        rest = [d for d in urgent if d not in direct] + easy
+        share = {h: [] for h in helpers}
+        done = {h: (i + 1) * _rows(topo, c, h) for i, h in enumerate(helpers)}
+        for d in rest:
+            best = min(helpers, key=lambda h: (done[h] + _rows(topo, h, d), helpers.index(h)))
+            share[best].append(d)
+            done[best] += _rows(topo, best, d)
         to = cores[(r - 1) % n]
-        if topo.may_write(c, to):
-            via = {"c0": far[0], "s0": far[1], "c1": None, "s1": None}
+        if not relayed[c]:
+            via = {"c0": None, "s0": None, "c1": None, "s1": None}
         else:
             via = {"c0": far[0], "s0": far[1], "c1": near[0], "s1": near[1]}
         plan.append({"core": c, "helpers": helpers, "direct": direct, "share": share, "to": to, "via": via})
@@ -98,9 +108,11 @@ def _helper(g, core, T, topo, plan):
             continue
         left = 0
         g.wait_ge(S.ssin0, _bits(topo.mask(p["core"], core)))
-        left += _fan(g, topo, core, p["share"][core], T.land[:, 4 * r:4 * r + 1], S.arr0, S.snt)
+        if p["share"][core]:
+            left += _fan(g, topo, core, p["share"][core], T.land[:, 4 * r:4 * r + 1], S.arr0, S.snt)
         g.wait_ge(S.ssin1, _bits(topo.mask(p["core"], core)))
-        left += _fan(g, topo, core, p["share"][core], T.land[:, 4 * r + 1:4 * r + 4], S.arr1, S.snt)
+        if p["share"][core]:
+            left += _fan(g, topo, core, p["share"][core], T.land[:, 4 * r + 1:4 * r + 4], S.arr1, S.snt)
         for name in PIECES:
             if p["via"][name] == core:
                 g.wait_ge(S["p_" + name], _bits(topo.mask(p["core"], core)))
@@ -143,7 +155,7 @@ def rank_program(g, core, T, topo):
     w1_load(s, 2)
     w1_load(y, 3)
 
-    cnt = float(n * NC)
+    cnt = float(n * NC) * SH * SH
     v.memset(T.land[:, 4 * n:W], EPS * cnt).then_inc(S.cst, 1)
     v.wait_ge(S.ld_x, 16)
     v.quantize_mx(T.xq[:], T.xsc[:], T.xb[:]).then_inc(S.q_x, 1)
@@ -157,7 +169,7 @@ def rank_program(g, core, T, topo):
         t.matmul_mx(T.zp[:, 512 * i:512 * i + NC], T.w1q[:, 128 * i:128 * i + 128], T.w1sc[:, 128 * i:128 * i + 128],
                     T.xq[:], T.xsc[:], True, True).then_inc(S["mm_%d" % i], 1)
         s.wait_ge(S["mm_%d" % i], 1)
-        s.activation(T.sqj[:, NC * i:NC * i + NC], T.zp[:, 512 * i:512 * i + NC], Act.Square,
+        s.activation(T.sqj[:, NC * i:NC * i + NC], T.zp[:, 512 * i:512 * i + NC], Act.Square, scale=SH,
                      accum_out=T.land[:, own + i:own + i + 1]).then_inc(S.sqa if i == 0 else S.sq, 1)
 
     g.wait_ge(S.sqa, 1)
@@ -169,45 +181,46 @@ def rank_program(g, core, T, topo):
     y.wait_ge(S.snt, left)
     y.dma_start(T.w2b[:], T.w2[:]).then_inc(S.ld_w2, 16)
 
-    inv = 1.0 / cnt
     s.wait_ge(S.sqa, 1)
     s.wait_ge(S.cst, 1)
     s.wait_ge(S.arr0, arr)
     s.activation(T.rj[:], T.land[:, 0:W:4], Act.Copy, accum_out=T.tot[:, 0:1]).then_inc(S.red0, 1)
     s.wait_ge(S.red0, 1)
-    s.activation(T.rt[:, 0:1], T.tot[:, 0:1], Act.Sqrt, scale=inv).then_inc(S.rts, 1)
+    s.activation(T.rt[:, 0:1], T.tot[:, 0:1], Act.Sqrt, scale=cnt).then_inc(S.rts0, 1)
+    v.wait_ge(S.red0, 1)
+    v.reciprocal(T.ra[:, 0:1], T.tot[:, 0:1]).then_inc(S.n0, 1)
+    s.wait_ge(S.rts0, 1)
+    s.wait_ge(S.n0, 1)
+    s.activation(T.sv[:, 0:1], T.rt[:, 0:1], Act.Copy, scale=T.ra[:, 0:1]).then_inc(S.s0r, 1)
     v.wait_ge(S.cst, 1)
     v.wait_ge(S.sq, G - 1)
     v.wait_ge(S.arr1, arr)
     for i in range(1, G):
         v.tensor_reduce(T.tot[:, i:i + 1], T.land[:, i:W:4], AxisListType.X, add).then_inc(S.redv, 1)
     s.wait_ge(S.redv, G - 1)
-    s.activation(T.rt[:, 1:G], T.tot[:, 1:G], Act.Sqrt, scale=inv).then_inc(S.rts, 1)
+    s.activation(T.rt[:, 1:G], T.tot[:, 1:G], Act.Sqrt, scale=cnt).then_inc(S.rts1, 1)
     v.wait_ge(S.redv, G - 1)
-    v.wait_ge(S.red0, 1)
-    v.reciprocal(T.ra[:], T.tot[:]).then_inc(S.n1, 1)
+    v.reciprocal(T.ra[:, 1:G], T.tot[:, 1:G]).then_inc(S.n1, 1)
+    s.wait_ge(S.s0r, 1)
+    s.activation(T.hb[:, 0:4 * NC:4], T.zp[:, 0:NC], Act.Copy, scale=T.sv[:, 0:1]).then_inc(S.h0, 1)
     v.wait_ge(S.n1, 1)
-    v.wait_ge(S.rts, 2)
-    v.tensor_tensor(T.uu[:], T.rt[:], T.ra[:], mult).then_inc(S.n2, 1)
-    v.wait_ge(S.n2, 1)
-    v.tensor_tensor(T.ww[:], T.rt[:], T.uu[:], mult).then_inc(S.n3, 1)
-    v.wait_ge(S.n3, 1)
-    v.tensor_scalar(T.tt[:], T.ww[:], -0.5 * cnt * cnt, 1.5 * cnt, mult, add).then_inc(S.n4, 1)
-    v.wait_ge(S.n4, 1)
-    v.tensor_tensor(T.sv[:], T.uu[:], T.tt[:], mult).then_inc(S.sready, 1)
+    v.wait_ge(S.rts1, 1)
+    v.tensor_tensor(T.sv[:, 1:G], T.rt[:, 1:G], T.ra[:, 1:G], mult).then_inc(S.sready, 1)
     v.wait_ge(S.sready, 1)
     s.wait_ge(S.sready, 1)
 
-    sent = 0
     for k in range(2):
-        for b in range(G):
+        for b in range(1, G):
             out = T.hb[:, 512 * k + b:512 * k + 512:4]
             z = T.zp[:, 512 * b + HALF * k:512 * b + HALF * k + HALF]
-            if b < 2:
+            if b == 1:
                 v.tensor_scalar(out, z, T.sv[:, b:b + 1], None, mult).then_inc(S["hv_%d" % k], 1)
             else:
                 s.activation(out, z, Act.Copy, scale=T.sv[:, b:b + 1]).then_inc(S["ha_%d" % k], 1)
-        v.wait_ge(S["hv_%d" % k], 2)
+    sent = 0
+    v.wait_ge(S.h0, 1)
+    for k in range(2):
+        v.wait_ge(S["hv_%d" % k], 1)
         v.wait_ge(S["ha_%d" % k], 2)
         v.quantize_mx(T.hq[:, HALF * k:HALF * k + HALF], T.hsc[:, HALF * k:HALF * k + HALF],
                       T.hb[:, 512 * k:512 * k + 512]).then_inc(S["q_h_%d" % k], 1)
@@ -219,8 +232,9 @@ def rank_program(g, core, T, topo):
                 dst, sem = p["to"], S["in%d" % k]
             sent += _send(g, topo, core, dst, _piece(T, "nq", "nsc", name), _piece(T, "hq", "hsc", name), sem, S.hsn)
 
+    y.wait_ge(S.h0, 1)
     for k in range(2):
-        y.wait_ge(S["hv_%d" % k], 2)
+        y.wait_ge(S["hv_%d" % k], 1)
         y.wait_ge(S["ha_%d" % k], 2)
     y.wait_ge(S.hsn, sent)
     y.dma_start(T.h[:], T.hb[:]).then_inc(S.st_h, 16)

from concourse.bass import DstId, RemoteDMATransfer
from concourse.mybir import dt, AluOpType, AxisListType, ActivationFunctionType

NC, G = 256, 4
EPS = 0.001
SIM_CORES = 128
HALF = NC // 2
NR = 12
SH = 2.0 ** -16
PIECES = ("c0", "s0", "c1", "s1")

SCRATCH = {
    "xb": ("sbuf", [128, 4 * NC], "bfloat16"),
    "w1b": ("sbuf", [128, G * 512], "bfloat16"),
    "w2b": ("sbuf", [128, 2 * 512], "bfloat16"),
    "xq": ("sbuf", [128, NC], "float8_e4m3fn_x4"), "xsc": ("sbuf", [128, NC], "uint8"),
    "w1q": ("sbuf", [128, G * 128], "float8_e4m3fn_x4"), "w1sc": ("sbuf", [128, G * 128], "uint8"),
    "w2q": ("sbuf", [128, 2 * 128], "float8_e4m3fn_x4"), "w2sc": ("sbuf", [128, 2 * 128], "uint8"),
    "zp": ("psum", [128, G * 512], "float32"),
    "yp": ("psum", [128, 2 * 512], "float32"),
    "sqj": ("sbuf", [128, G * NC], "float32"),
    "land": ("sbuf", [128, 4 * (NR + 1)], "float32"),
    "rj": ("sbuf", [128, NR + 1], "float32"),
    "tot": ("sbuf", [128, G], "float32"),
    "rt": ("sbuf", [128, G], "float32"),
    "ra": ("sbuf", [128, G], "float32"),
    "sv": ("sbuf", [128, G], "float32"),
    "hb": ("sbuf", [128, 4 * NC], "bfloat16"),
    "hq": ("sbuf", [128, NC], "float8_e4m3fn_x4"), "hsc": ("sbuf", [128, NC], "uint8"),
    "nq": ("sbuf", [128, NC], "float8_e4m3fn_x4"), "nsc": ("sbuf", [128, NC], "uint8"),
    "ysb": ("sbuf", [128, NC], "float32"),
}
SEMAPHORES = (["ld_x", "ld_w2", "q_x", "q_w2", "sqa", "sq", "ssin0", "ssin1", "snt", "arr0", "arr1", "cst", "red0", "redv",
               "rts0", "rts1", "n0", "n1", "s0r", "h0", "sready", "hsn", "in0", "in1", "y0", "y1", "yc0", "yc1",
               "st_h", "st_y0", "st_y1"]
              + ["p_" + k for k in PIECES]
              + ["ld_w1_%d" % i for i in range(G)] + ["q_w1_%d" % i for i in range(G)] + ["mm_%d" % i for i in range(G)]
              + ["hv_%d" % k for k in range(2)] + ["ha_%d" % k for k in range(2)] + ["q_h_%d" % k for k in range(2)])


def _bits(m):
    return bin(m).count("1")


def _rows(topo, a, b):
    return 128 // _bits(topo.mask(a, b))


def _plan(T, topo):
    cores = list(T.cores)
    n = len(cores)
    relayed = {c: not topo.may_write(c, cores[(r - 1) % n]) for r, c in enumerate(cores)}
    plan = []
    for r, c in enumerate(cores):
        others = [d for d in cores if d != c]
        ports = [k for k in range(SIM_CORES)
                 if topo.chip(k) == topo.chip(c) and k not in cores and all(topo.may_write(k, d) for d in others)]
        near = [k for k in ports if topo.die(k) == topo.die(c)]
        far = [k for k in ports if topo.die(k) != topo.die(c)]
        helpers = near + far
        urgent = [d for d in others if relayed[d]]
        easy = [d for d in others if not relayed[d]]
        direct = [d for d in urgent if topo.may_write(c, d)][:3]
        rest = [d for d in urgent if d not in direct] + easy
        share = {h: [] for h in helpers}
        done = {h: (i + 1) * _rows(topo, c, h) for i, h in enumerate(helpers)}
        for d in rest:
            best = min(helpers, key=lambda h: (done[h] + _rows(topo, h, d), helpers.index(h)))
            share[best].append(d)
            done[best] += _rows(topo, best, d)
        to = cores[(r - 1) % n]
        if not relayed[c]:
            via = {"c0": None, "s0": None, "c1": None, "s1": None}
        else:
            via = {"c0": far[0], "s0": far[1], "c1": near[0], "s1": near[1]}
        plan.append({"core": c, "helpers": helpers, "direct": direct, "share": share, "to": to, "via": via})
    return plan


def _fan(g, topo, src_core, dsts, ap, remote_sem, local_sem):
    m = topo.mask(src_core, dsts[0])
    for d in dsts:
        m &= topo.mask(src_core, d)
    ids = [DstId(rid=topo.addr(d)[0], pnc=topo.addr(d)[1]) for d in dsts]
    g.remote_dma_fused([RemoteDMATransfer(dst_ids=ids, dma_engine_mask=m, remote_sem=remote_sem,
                                          srcs=[ap], dsts=[ap for _ in dsts])], local_sem=local_sem)
    return _bits(m)


def _send(g, topo, src_core, dst_core, out_ap, in_ap, remote_sem, local_sem):
    rid, pid = topo.addr(dst_core)[:2]
    m = topo.mask(src_core, dst_core)
    g.remote_dma(out_ap, in_ap, remote_sem, local_sem, pid, rid, m)
    return _bits(m)


def _piece(T, buf_q, buf_s, name):
    k = int(name[1])
    if name[0] == "c":
        return T[buf_q][:, HALF * k:HALF * k + HALF].bitcast(dt.uint8)
    return T[buf_s][:, HALF * k:HALF * k + HALF]


def _helper(g, core, T, topo, plan):
    S = T.sem
    for r, p in enumerate(plan):
        if core not in p["helpers"]:
            continue
        left = 0
        g.wait_ge(S.ssin0, _bits(topo.mask(p["core"], core)))
        if p["share"][core]:
            left += _fan(g, topo, core, p["share"][core], T.land[:, 4 * r:4 * r + 1], S.arr0, S.snt)
        g.wait_ge(S.ssin1, _bits(topo.mask(p["core"], core)))
        if p["share"][core]:
            left += _fan(g, topo, core, p["share"][core], T.land[:, 4 * r + 1:4 * r + 4], S.arr1, S.snt)
        for name in PIECES:
            if p["via"][name] == core:
                g.wait_ge(S["p_" + name], _bits(topo.mask(p["core"], core)))
                ap = _piece(T, "nq", "nsc", name)
                left += _send(g, topo, core, p["to"], ap, ap, S["in" + name[1]], S.snt)
        g.wait_ge(S.snt, left)


def rank_program(g, core, T, topo):
    plan = _plan(T, topo)
    rank = T.rank_of(core)
    if rank is None:
        _helper(g, core, T, topo, plan)
        return
    S = T.sem
    p = plan[rank]
    n = len(plan)
    v, s, t, y = g.vector, g.scalar, g.tensor, g.sync
    mult, add = AluOpType.mult, AluOpType.add
    Act = ActivationFunctionType
    W = 4 * (n + 1)

    arr = 0
    for q in plan:
        if core in q["direct"]:
            arr += _bits(topo.mask(q["core"], core))
        for h in q["helpers"]:
            if core in q["share"][h]:
                arr += _bits(topo.mask(h, core))
    src = plan[(rank + 1) % n]
    got = [0, 0]
    for name in PIECES:
        got[int(name[1])] += _bits(topo.mask(src["via"][name] if src["via"][name] is not None else src["core"], core))

    def w1_load(q, i):
        q.dma_start(T.w1b[:, 512 * i:512 * i + 512], T.w1[:, 512 * i:512 * i + 512]).then_inc(S["ld_w1_%d" % i], 16)
    y.dma_start(T.xb[:], T.x[:]).then_inc(S.ld_x, 16)
    w1_load(s, 0)
    w1_load(y, 1)
    w1_load(s, 2)
    w1_load(y, 3)

    cnt = float(n * NC) * SH * SH
    v.memset(T.land[:, 4 * n:W], EPS * cnt).then_inc(S.cst, 1)
    v.wait_ge(S.ld_x, 16)
    v.quantize_mx(T.xq[:], T.xsc[:], T.xb[:]).then_inc(S.q_x, 1)
    t.wait_ge(S.q_x, 1)
    own = 4 * rank
    for i in range(G):
        v.wait_ge(S["ld_w1_%d" % i], 16)
        v.quantize_mx(T.w1q[:, 128 * i:128 * i + 128], T.w1sc[:, 128 * i:128 * i + 128],
                      T.w1b[:, 512 * i:512 * i + 512]).then_inc(S["q_w1_%d" % i], 1)
        t.wait_ge(S["q_w1_%d" % i], 1)
        t.matmul_mx(T.zp[:, 512 * i:512 * i + NC], T.w1q[:, 128 * i:128 * i + 128], T.w1sc[:, 128 * i:128 * i + 128],
                    T.xq[:], T.xsc[:], True, True).then_inc(S["mm_%d" % i], 1)
        s.wait_ge(S["mm_%d" % i], 1)
        s.activation(T.sqj[:, NC * i:NC * i + NC], T.zp[:, 512 * i:512 * i + NC], Act.Square, scale=SH,
                     accum_out=T.land[:, own + i:own + i + 1]).then_inc(S.sqa if i == 0 else S.sq, 1)

    g.wait_ge(S.sqa, 1)
    left = _fan(g, topo, core, p["helpers"], T.land[:, own:own + 1], S.ssin0, S.snt)
    left += _fan(g, topo, core, p["direct"], T.land[:, own:own + 1], S.arr0, S.snt)
    g.wait_ge(S.sq, G - 1)
    left += _fan(g, topo, core, p["helpers"], T.land[:, own + 1:own + 4], S.ssin1, S.snt)
    left += _fan(g, topo, core, p["direct"], T.land[:, own + 1:own + 4], S.arr1, S.snt)
    y.wait_ge(S.snt, left)
    y.dma_start(T.w2b[:], T.w2[:]).then_inc(S.ld_w2, 16)

    s.wait_ge(S.sqa, 1)
    s.wait_ge(S.cst, 1)
    s.wait_ge(S.arr0, arr)
    s.activation(T.rj[:], T.land[:, 0:W:4], Act.Copy, accum_out=T.tot[:, 0:1]).then_inc(S.red0, 1)
    s.wait_ge(S.red0, 1)
    s.activation(T.rt[:, 0:1], T.tot[:, 0:1], Act.Sqrt, scale=cnt).then_inc(S.rts0, 1)
    v.wait_ge(S.red0, 1)
    v.reciprocal(T.ra[:, 0:1], T.tot[:, 0:1]).then_inc(S.n0, 1)
    s.wait_ge(S.rts0, 1)
    s.wait_ge(S.n0, 1)
    s.activation(T.sv[:, 0:1], T.rt[:, 0:1], Act.Copy, scale=T.ra[:, 0:1]).then_inc(S.s0r, 1)
    v.wait_ge(S.cst, 1)
    v.wait_ge(S.sq, G - 1)
    v.wait_ge(S.arr1, arr)
    for i in range(1, G):
        v.tensor_reduce(T.tot[:, i:i + 1], T.land[:, i:W:4], AxisListType.X, add).then_inc(S.redv, 1)
    s.wait_ge(S.redv, G - 1)
    s.activation(T.rt[:, 1:G], T.tot[:, 1:G], Act.Sqrt, scale=cnt).then_inc(S.rts1, 1)
    v.wait_ge(S.redv, G - 1)
    v.reciprocal(T.ra[:, 1:G], T.tot[:, 1:G]).then_inc(S.n1, 1)
    s.wait_ge(S.s0r, 1)
    s.activation(T.hb[:, 0:4 * NC:4], T.zp[:, 0:NC], Act.Copy, scale=T.sv[:, 0:1]).then_inc(S.h0, 1)
    v.wait_ge(S.n1, 1)
    v.wait_ge(S.rts1, 1)
    v.tensor_tensor(T.sv[:, 1:G], T.rt[:, 1:G], T.ra[:, 1:G], mult).then_inc(S.sready, 1)
    v.wait_ge(S.sready, 1)
    s.wait_ge(S.sready, 1)

    for k in range(2):
        for b in range(1, G):
            out = T.hb[:, 512 * k + b:512 * k + 512:4]
            z = T.zp[:, 512 * b + HALF * k:512 * b + HALF * k + HALF]
            if b == 1:
                v.tensor_scalar(out, z, T.sv[:, b:b + 1], None, mult).then_inc(S["hv_%d" % k], 1)
            else:
                s.activation(out, z, Act.Copy, scale=T.sv[:, b:b + 1]).then_inc(S["ha_%d" % k], 1)
    sent = 0
    v.wait_ge(S.h0, 1)
    for k in range(2):
        v.wait_ge(S["hv_%d" % k], 1)
        v.wait_ge(S["ha_%d" % k], 2)
        v.quantize_mx(T.hq[:, HALF * k:HALF * k + HALF], T.hsc[:, HALF * k:HALF * k + HALF],
                      T.hb[:, 512 * k:512 * k + 512]).then_inc(S["q_h_%d" % k], 1)
        g.wait_ge(S["q_h_%d" % k], 1)
        for name in ("c%d" % k, "s%d" % k):
            if p["via"][name] is not None:
                dst, sem = p["via"][name], S["p_" + name]
            else:
                dst, sem = p["to"], S["in%d" % k]
            sent += _send(g, topo, core, dst, _piece(T, "nq", "nsc", name), _piece(T, "hq", "hsc", name), sem, S.hsn)

    y.wait_ge(S.h0, 1)
    for k in range(2):
        y.wait_ge(S["hv_%d" % k], 1)
        y.wait_ge(S["ha_%d" % k], 2)
    y.wait_ge(S.hsn, sent)
    y.dma_start(T.h[:], T.hb[:]).then_inc(S.st_h, 16)

    v.wait_ge(S.ld_w2, 16)
    for i in range(2):
        v.quantize_mx(T.w2q[:, 128 * i:128 * i + 128], T.w2sc[:, 128 * i:128 * i + 128],
                      T.w2b[:, 512 * i:512 * i + 512]).then_inc(S.q_w2, 1)
    t.wait_ge(S.q_w2, 2)
    for k in range(2):
        t.wait_ge(S["q_h_%d" % k], 1)
        t.matmul_mx(T.yp[:, 512 * k:512 * k + HALF], T.w2q[:, 0:128], T.w2sc[:, 0:128],
                    T.hq[:, HALF * k:HALF * k + HALF], T.hsc[:, HALF * k:HALF * k + HALF], True, False)
    for k in range(2):
        t.wait_ge(S["in%d" % k], got[k])
        t.matmul_mx(T.yp[:, 512 * k:512 * k + HALF], T.w2q[:, 128:256], T.w2sc[:, 128:256],
                    T.nq[:, HALF * k:HALF * k + HALF], T.nsc[:, HALF * k:HALF * k + HALF], False, True).then_inc(S["y%d" % k], 1)
    v.wait_ge(S.y0, 1)
    v.tensor_copy(T.ysb[:, 0:HALF], T.yp[:, 0:HALF]).then_inc(S.yc0, 1)
    y.wait_ge(S.yc0, 1)
    y.dma_start(T.y[:, 0:HALF], T.ysb[:, 0:HALF]).then_inc(S.st_y0, 16)
    s.wait_ge(S.y1, 1)
    s.activation(T.ysb[:, HALF:NC], T.yp[:, 512:512 + HALF], Act.Copy).then_inc(S.yc1, 1)
    s.wait_ge(S.yc1, 1)
    s.dma_start(T.y[:, HALF:NC], T.ysb[:, HALF:NC]).then_inc(S.st_y1, 16)
    y.wait_ge(S.st_h, 16)
    y.wait_ge(S.st_y0, 16)
    s.wait_ge(S.st_y1, 16)
